import numpy as np, ml_dtypes
CORES = [12,28,44,60,3,19,35,51]
N = 8
import mx_ref
NC, G = 512, 2
C = np.float32(0.043)
BF = ml_dtypes.bfloat16
def cut(t, i, w=512):
    return t[:, w * i:w * i + w]
def tile(rs):
    return np.stack(rs, axis=2).reshape(128, -1).astype(BF)
def layer(w, X):
    out = []
    for i in range(G):
        for t in range(len(X)):
            p = mx_ref.matmul(mx_ref.quantize(cut(w, len(X) * i + t)), X[t])
            z = p if t == 0 else z + p
        out.append(z)
    return out
def act(Z):
    return [np.maximum(s * z, 0) * C for z in Z for s in (1, -1)]
def turned(R):
    return [np.concatenate([R[b][:, 128 * t:128 * t + 128].T for b in range(4)], axis=1) for t in range(4)]
def setup_inputs(rng):
    def f(*shape):
        return mx_ref.flush((rng.standard_normal(shape, dtype=np.float32) * np.exp2(rng.integers(-2, 3, shape[:-1] + (1,)))).astype(BF))
    return {"x": f(N, 128, 4 * 512), "w1": f(N, 128, G * 512), "w2": f(N, 128, 512), "e": f(N, 128, 4 * NC)}
def setup_inputs_blocks(rng):
    d = setup_inputs(rng)
    for k in ("x", "w1", "w2", "e"): d[k] = mx_ref.spread(d[k], rng, 4)
    return d
def setup_inputs_wide(rng):
    d = setup_inputs(rng)
    for k in ("x", "w1", "w2", "e"): d[k] = mx_ref.flush((d[k].astype(np.float32) * np.exp2(rng.integers(-6, 7, (N, 1, 1))).astype(np.float32)).astype(BF))
    return d
def setup_inputs_zeros(rng):
    d = setup_inputs(rng); v = d["x"].reshape(N, 128, -1, 4).copy()
    v[np.broadcast_to((rng.random((N, 1, v.shape[2], 1)) < 0.33), v.shape)] = 0
    d["x"] = v.reshape(d["x"].shape)
    return d
def reference(x, w1, w2, e):
    R = [act(layer(w1[j], [mx_ref.quantize(x[j])])) for j in range(N)]
    H = [mx_ref.quantize(tile(R[j])) for j in range(N)]
    K = [tile(turned(R[j])) for j in range(N)]
    y = np.zeros((N, 128, 512), np.float32); z = np.zeros((N, 128, 4 * NC), np.float32)
    for r in range(N):
        y[r] = mx_ref.matmul(mx_ref.quantize(w2[r]), H[(r - 1) % N]); qe = mx_ref.quantize(e[r])
        for b in range(4):
            z[r][:, NC * b:NC * b + NC] = mx_ref.matmul(mx_ref.quantize(cut(K[(r + 1) % N], b)), qe)
    return {"y": y, "z": z}

@@ -1,0 +1,245 @@
+from concourse.mybir import dt, AluOpType, ActivationFunctionType
+
+CODES, BF, F32, U8 = "float8_e4m3fn_x4", "bfloat16", "float32", "uint8"
+SCRATCH = {
+    "xb": ("sbuf", [128, 2048], BF), "w1b": ("sbuf", [128, 1024], BF),
+    "w2b": ("sbuf", [128, 512], BF), "eb": ("sbuf", [128, 2048], BF),
+    "qx": ("sbuf", [128, 512], CODES), "sx": ("sbuf", [128, 512], U8),
+    "qw1": ("sbuf", [128, 256], CODES), "sw1": ("sbuf", [128, 256], U8),
+    "qw2": ("sbuf", [128, 128], CODES), "sw2": ("sbuf", [128, 128], U8),
+    "qe": ("sbuf", [128, 512], CODES), "se": ("sbuf", [128, 512], U8),
+    "ht": ("sbuf", [128, 2048], BF), "kt": ("sbuf", [128, 2048], BF),
+    "qh": ("sbuf", [128, 512], CODES), "sh": ("sbuf", [128, 512], U8),
+    "qk": ("sbuf", [128, 512], CODES), "sk": ("sbuf", [128, 512], U8),
+    "rh": ("sbuf", [128, 512], CODES), "rhs": ("sbuf", [128, 512], U8),
+    "rk": ("sbuf", [128, 512], CODES), "rks": ("sbuf", [128, 512], U8),
+    "yb": ("sbuf", [128, 512], F32), "zb": ("sbuf", [128, 2048], F32),
+    "ps": ("psum", [128, 4096], F32),
+}
+PIECES = {"hc0": (0, 128, ["qh0"]), "hc1": (128, 512, ["qh1"]), "hs": (0, 512, ["qh0", "qh1"]),
+          "kc0": (0, 256, ["qk0"]), "kc1": (256, 512, ["qk1"]), "ks": (0, 512, ["qk0", "qk1"])}
+POS = {0: 0, 2: 1, 1: 2, 3: 3}
+C = 0.043
+SEMAPHORES = (["lx0", "lx1", "lx2", "lw1", "lw2", "le", "qx0", "qx1", "qx2", "qw1", "qw2", "qe"]
+              + ["mh0a", "mh0b", "mk0", "mk1", "mk2", "mk3a", "mk3b", "mh1a", "mh1b"]
+              + ["eh0", "eh1", "ekp", "ekm", "et2", "qh0", "qh1", "qk0", "qk1"]
+              + ["mz0", "mz1", "mz2", "mz3", "my", "ez0", "ez1", "ez2", "ez3", "ey", "st", "sent"]
+              + ["a" + p for p in PIECES])
+
+
+def _mask(topo, route, i):
+    return topo.mask(route[i], route[i + 1]) & topo.mask(route[i], route[-1])
+
+
+def _routes(T, topo):
+    n, out = len(T.cores), []
+    for r in range(n):
+        src, hd, kd = T.cores[r], T.cores[(r + 1) % n], T.cores[(r - 1) % n]
+
+        def way(dst):
+            if topo.may_write(src, dst):
+                return [src, dst]
+            return [src, [c for c in range(64) if c not in T.cores and topo.chip(c) == topo.chip(src)
+                          and topo.die(c) == topo.die(src) and topo.may_write(c, dst)][0], dst]
+
+        hw, kw = way(hd), way(kd)
+        first = [("hc0", hw[:1] + kw[1:-1] + hw[-1:] if len(kw) > 2 else hw)]
+        rest = [("hc1", hw), ("hs", hw)]
+        kk = [(p, kw) for p in ("kc0", "ks", "kc1")]
+        out.append(first + (rest + kk if len(hw) > 2 else kk + rest))
+    return out
+
+
+def _send(g, T, topo, route, i, p):
+    a, b, _ = PIECES[p]
+    t = p[0]
+    if p[1] == "c":
+        s = T[("r" if i else "q") + t][:, a:b].bitcast(dt.uint8)
+        d = T["r" + t][:, a:b].bitcast(dt.uint8)
+    else:
+        s = T["r" + t + "s" if i else "s" + t][:, a:b]
+        d = T["r" + t + "s"][:, a:b]
+    rid, pid, _ = topo.addr(route[i + 1])
+    m = _mask(topo, route, i)
+    g.remote_dma(d, s, T.sem["a" + p], T.sem.sent, pid, rid, m)
+    return m.bit_count()
+
+
+def rank_program(g, core, T, topo):
+    routes = _routes(T, topo)
+    arrive = {}
+    for sends in routes:
+        for p, route in sends:
+            if core in route[1:]:
+                arrive[p] = _mask(topo, route, route.index(core) - 1).bit_count()
+    rank = T.rank_of(core)
+    if rank is None:
+        sent = 0
+        for sends in routes:
+            for p, route in sends:
+                if core in route:
+                    g.wait_ge(T.sem["a" + p], arrive[p])
+                    sent += _send(g, T, topo, route, 1, p)
+        if sent:
+            g.wait_ge(T.sem.sent, sent)
+        return
+    sends = routes[rank]
+    hfirst = sends[1][0] == "hc1"
+    S = T.sem
+    V, A, PE, SY = g.vector, g.scalar, g.tensor, g.sync
+
+    SY.dma_start(T.w1b[:], T.w1[:]).then_inc(S.lw1, 16)
+    for a, b, e in ((0, 512, S.lx0), (512, 1024, S.lx1), (1024, 2048, S.lx2)):
+        SY.dma_start(T.xb[:, a:b], T.x[:, a:b]).then_inc(e, 16)
+    SY.wait_ge(S.lx0, 16)
+    SY.dma_start(T.eb[:], T.e[:]).then_inc(S.le, 16)
+    SY.dma_start(T.w2b[:], T.w2[:]).then_inc(S.lw2, 16)
+
+    def quant(sem, n, q, s, src, a, b, done):
+        V.wait_ge(sem, n)
+        V.quantize_mx(q[:, a:b], s[:, a:b], src[:, 4 * a:4 * b]).then_inc(done, 1)
+
+    def bank(i, n):
+        return T.ps[:, 512 * i:512 * i + n]
+
+    def mm(i, n, l, ls, la, r, rs, ra, done):
+        PE.matmul_mx(bank(i, n), l[:, la:la + 128], ls[:, la:la + 128], r[:, ra:ra + n], rs[:, ra:ra + n],
+                     True, True).then_inc(done, 1)
+
+    def vrelu(out, i, n, sign, done):
+        V.tensor_scalar(out, bank(i, n), sign * C, 0.0, AluOpType.mult, AluOpType.max).then_inc(done, 1)
+
+    def arelu(out, i, n, sign, done):
+        A.activation(out, bank(i, n), ActivationFunctionType.Relu, scale=sign * C).then_inc(done, 1)
+
+    def hcols(a, b, k):
+        return T.ht[:, 4 * a + k:4 * b:4]
+
+    def kcols(half, t, i=None):
+        a = 1024 * half + (0 if i is None else 512 * i)
+        return T.kt[:, a + t:a + (1024 if i is None else 512):4]
+
+    def hmm(a, b, ba, bb, sa, sb):
+        mm(ba, b - a, T.qw1, T.sw1, 0, T.qx, T.sx, a, sa)
+        mm(bb, b - a, T.qw1, T.sw1, 128, T.qx, T.sx, a, sb)
+
+    def h1mm():
+        PE.wait_ge(S.eh0, 4)
+        hmm(128, 512, 7, 6, S.mh1a, S.mh1b)
+
+    def kmm(i, n, t, ra, done):
+        mm(i, n, T.qx, T.sx, 128 * t, T.qw1, T.sw1, ra, done)
+
+    PE.wait_ge(S.qx0, 1)
+    PE.wait_ge(S.qw1, 1)
+    hmm(0, 128, 5, 6, S.mh0a, S.mh0b)
+    if hfirst:
+        PE.wait_ge(S.qx1, 1)
+        PE.wait_ge(S.qx2, 1)
+        h1mm()
+    kmm(0, 256, 0, 0, S.mk0)
+    PE.wait_ge(S.qx1, 1)
+    kmm(1, 256, 1, 0, S.mk1)
+    PE.wait_ge(S.qx2, 1)
+    kmm(2, 256, 2, 0, S.mk2)
+    kmm(3, 128, 3, 0, S.mk3a)
+    kmm(4, 128, 3, 128, S.mk3b)
+    if not hfirst:
+        h1mm()
+
+    def vh1():
+        V.wait_ge(S.mh1a, 1)
+        vrelu(hcols(128, 512, 0), 7, 384, 1, S.eh1)
+        vrelu(hcols(128, 512, 1), 7, 384, -1, S.eh1)
+        quant(S.eh1, 4, T.qh, T.sh, T.ht, 128, 512, S.qh1)
+
+    quant(S.lw1, 16, T.qw1, T.sw1, T.w1b, 0, 256, S.qw1)
+    quant(S.lx0, 16, T.qx, T.sx, T.xb, 0, 128, S.qx0)
+    V.wait_ge(S.mh0a, 1)
+    vrelu(hcols(0, 128, 0), 5, 128, 1, S.eh0)
+    vrelu(hcols(0, 128, 1), 5, 128, -1, S.eh0)
+    quant(S.lx1, 16, T.qx, T.sx, T.xb, 128, 256, S.qx1)
+    quant(S.eh0, 4, T.qh, T.sh, T.ht, 0, 128, S.qh0)
+    quant(S.lx2, 16, T.qx, T.sx, T.xb, 256, 512, S.qx2)
+    if hfirst:
+        vh1()
+    V.wait_ge(S.mk2, 1)
+    vrelu(kcols(0, 2), 2, 256, 1, S.et2)
+    V.wait_ge(S.mk3a, 1)
+    vrelu(kcols(0, 3, 0), 3, 128, 1, S.ekp)
+    V.wait_ge(S.et2, 1)
+    quant(S.ekp, 4, T.qk, T.sk, T.kt, 0, 256, S.qk0)
+    vrelu(kcols(1, 3, 0), 3, 128, -1, S.ekm)
+    quant(S.ekm, 5, T.qk, T.sk, T.kt, 256, 512, S.qk1)
+    if not hfirst:
+        vh1()
+    quant(S.le, 16, T.qe, T.se, T.eb, 0, 512, S.qe)
+    quant(S.lw2, 16, T.qw2, T.sw2, T.w2b, 0, 128, S.qw2)
+
+    def ah1():
+        A.wait_ge(S.mh1b, 1)
+        arelu(hcols(128, 512, 2), 6, 384, 1, S.eh1)
+        arelu(hcols(128, 512, 3), 6, 384, -1, S.eh1)
+
+    A.wait_ge(S.mh0b, 1)
+    arelu(hcols(0, 128, 2), 6, 128, 1, S.eh0)
+    arelu(hcols(0, 128, 3), 6, 128, -1, S.eh0)
+    if hfirst:
+        ah1()
+    for t, m in ((0, S.mk0), (1, S.mk1)):
+        A.wait_ge(m, 1)
+        arelu(kcols(0, t), t, 256, 1, S.ekp)
+        arelu(kcols(1, t), t, 256, -1, S.ekm)
+    A.wait_ge(S.mk3b, 1)
+    arelu(kcols(0, 3, 1), 4, 128, 1, S.ekp)
+    A.wait_ge(S.et2, 1)
+    arelu(kcols(1, 2), 2, 256, -1, S.ekm)
+    arelu(kcols(1, 3, 1), 4, 128, -1, S.ekm)
+    if not hfirst:
+        ah1()
+
+    sent = 0
+    for p, route in sends:
+        for e in PIECES[p][2]:
+            g.wait_ge(S[e], 1)
+        sent += _send(g, T, topo, route, 0, p)
+    g.wait_ge(S.sent, sent)
+
+    def do_y():
+        PE.wait_ge(S.qw2, 1)
+        PE.wait_ge(S.eh0, 4)
+        for p in ("hc0", "hc1", "hs"):
+            PE.wait_ge(S["a" + p], arrive[p])
+        mm(5, 512, T.qw2, T.sw2, 0, T.rh, T.rhs, 0, S.my)
+        V.wait_ge(S.my, 1)
+        V.tensor_copy(T.yb[:], bank(5, 512)).then_inc(S.ey, 1)
+        SY.wait_ge(S.ey, 1)
+        SY.dma_start(T.y[:], T.yb[:]).then_inc(S.st, 16)
+
+    def do_z():
+        PE.wait_ge(S.qe, 1)
+        PE.wait_ge(S.ekm, 5)
+        PE.wait_ge(S.ekp, 4)
+        PE.wait_ge(S.et2, 1)
+        for pieces, blocks in ((("kc0", "ks"), (0, 2)), (("kc1",), (1, 3))):
+            for p in pieces:
+                PE.wait_ge(S["a" + p], arrive[p])
+            for i, b in enumerate(blocks):
+                m, e = S["mz%d" % b], S["ez%d" % b]
+                mm(1 + POS[b], 512, T.rk, T.rks, 128 * POS[b], T.qe, T.se, 0, m)
+                (V, A)[i].wait_ge(m, 1)
+                dst = T.zb[:, 512 * b:512 * b + 512]
+                if i == 0:
+                    V.tensor_copy(dst, bank(1 + POS[b], 512)).then_inc(e, 1)
+                else:
+                    A.activation(dst, bank(1 + POS[b], 512), ActivationFunctionType.Copy).then_inc(e, 1)
+                SY.wait_ge(e, 1)
+                SY.dma_start(T.z[:, 512 * b:512 * b + 512], dst).then_inc(S.st, 16)
+
+    if [len(route) for p, route in routes[(rank + 1) % len(T.cores)] if p == "ks"][0] > 2:
+        do_y()
+        do_z()
+    else:
+        do_z()
+        do_y()
+    SY.wait_ge(S.st, 80)

@@ -16,37 +16,46 @@ SCRATCH = {
     "yb": ("sbuf", [128, 512], F32), "zb": ("sbuf", [128, 2048], F32),
     "ps": ("psum", [128, 4096], F32),
 }
-PIECES = {"hc0": (0, 128, ["qh0"]), "hc1": (128, 512, ["qh1"]), "hs": (0, 512, ["qh0", "qh1"]),
-          "kc0": (0, 256, ["qk0"]), "kc1": (256, 512, ["qk1"]), "ks": (0, 512, ["qk0", "qk1"])}
+PIECES = {"hc0": (0, 128, ["qh0"]), "hc1": (128, 512, ["qh1"]), "hc2": (128, 384, ["qh1"]), "hc3": (384, 512, ["qh1"]),
+          "hs": (0, 512, ["qh0", "qh1"]), "hs0": (0, 128, ["qh0"]), "hs1": (128, 512, ["qh1"]),
+          "kc0": (0, 256, ["qk0"]), "kc1": (256, 512, ["qk1"]), "ks": (0, 512, ["qk0", "qk1"]),
+          "ks0": (0, 256, ["qk0"]), "ks1": (256, 512, ["qk1"])}
 POS = {0: 0, 2: 1, 1: 2, 3: 3}
 C = 0.043
-SEMAPHORES = (["lx0", "lx1", "lx2", "lw1", "lw2", "le", "qx0", "qx1", "qx2", "qw1", "qw2", "qe"]
+SEMAPHORES = (["lx0", "lx1", "lx2", "lw1", "lw2", "le", "qx0", "qx1", "qx2", "qx3", "qw1", "qw2", "qe"]
               + ["mh0a", "mh0b", "mk0", "mk1", "mk2", "mk3a", "mk3b", "mh1a", "mh1b"]
               + ["eh0", "eh1", "ekp", "ekm", "et2", "qh0", "qh1", "qk0", "qk1"]
-              + ["mz0", "mz1", "mz2", "mz3", "my", "ez0", "ez1", "ez2", "ez3", "ey", "st", "sent"]
+              + [a + b for a in ("mz", "nz", "ez") for b in "0123"] + ["my", "ny", "ey", "st", "sent"]
               + ["a" + p for p in PIECES])
 
 
-def _mask(topo, route, i):
-    return topo.mask(route[i], route[i + 1]) & topo.mask(route[i], route[-1])
+def _mask(topo, route, i, p):
+    m, out = topo.mask(route[i], route[i + 1]), topo.mask(route[i], route[-1])
+    if p in ("hc0", "hs0"):
+        return m & out
+    if p in ("hc3", "hs") and m != out:
+        return m & ~out
+    return m
 
 
 def _routes(T, topo):
     n, out = len(T.cores), []
     for r in range(n):
         src, hd, kd = T.cores[r], T.cores[(r + 1) % n], T.cores[(r - 1) % n]
-
-        def way(dst):
-            if topo.may_write(src, dst):
-                return [src, dst]
-            return [src, [c for c in range(64) if c not in T.cores and topo.chip(c) == topo.chip(src)
-                          and topo.die(c) == topo.die(src) and topo.may_write(c, dst)][0], dst]
-
-        hw, kw = way(hd), way(kd)
-        first = [("hc0", hw[:1] + kw[1:-1] + hw[-1:] if len(kw) > 2 else hw)]
-        rest = [("hc1", hw), ("hs", hw)]
-        kk = [(p, kw) for p in ("kc0", "ks", "kc1")]
-        out.append(first + (rest + kk if len(hw) > 2 else kk + rest))
+        far = [d for d in (hd, kd) if not topo.may_write(src, d)]
+        a, b = [[c for c in range(64) if c not in T.cores and topo.chip(c) == topo.chip(src)
+                 and (topo.die(c) == topo.die(src)) == same and all(topo.may_write(c, d) for d in far + [hd])][0]
+                for same in (True, False)]
+        direct, other, near = [src, hd], [src, b, hd], [src, a, hd]
+        if far == [kd]:
+            out.append([("hs0", near), ("hc0", other), ("kc0", [src, a, kd]), ("ks0", [src, a, kd]), ("kc1", [src, b, kd]),
+                        ("ks1", [src, b, kd]), ("hc3", other), ("hs1", other), ("hc2", direct)])
+        elif far == [hd]:
+            out.append([("hs0", other), ("hc0", near), ("kc0", [src, kd]), ("ks", [src, kd]), ("kc1", [src, kd]),
+                        ("hc1", near), ("hs1", other)])
+        else:
+            out.append([("hc0", other), ("kc0", [src, kd]), ("ks", [src, kd]), ("kc1", [src, kd]),
+                        ("hc3", other), ("hs", other), ("hc2", direct)])
     return out
 
 
@@ -60,7 +69,7 @@ def _send(g, T, topo, route, i, p):
         s = T["r" + t + "s" if i else "s" + t][:, a:b]
         d = T["r" + t + "s"][:, a:b]
     rid, pid, _ = topo.addr(route[i + 1])
-    m = _mask(topo, route, i)
+    m = _mask(topo, route, i, p)
     g.remote_dma(d, s, T.sem["a" + p], T.sem.sent, pid, rid, m)
     return m.bit_count()
 
@@ -71,7 +80,7 @@ def rank_program(g, core, T, topo):
     for sends in routes:
         for p, route in sends:
             if core in route[1:]:
-                arrive[p] = _mask(topo, route, route.index(core) - 1).bit_count()
+                arrive[p] = _mask(topo, route, route.index(core) - 1, p).bit_count()
     rank = T.rank_of(core)
     if rank is None:
         sent = 0
@@ -83,8 +92,6 @@ def rank_program(g, core, T, topo):
         if sent:
             g.wait_ge(T.sem.sent, sent)
         return
-    sends = routes[rank]
-    hfirst = sends[1][0] == "hc1"
     S = T.sem
     V, A, PE, SY = g.vector, g.scalar, g.tensor, g.sync
 
@@ -123,35 +130,22 @@ def rank_program(g, core, T, topo):
         mm(ba, b - a, T.qw1, T.sw1, 0, T.qx, T.sx, a, sa)
         mm(bb, b - a, T.qw1, T.sw1, 128, T.qx, T.sx, a, sb)
 
-    def h1mm():
-        PE.wait_ge(S.eh0, 4)
-        hmm(128, 512, 7, 6, S.mh1a, S.mh1b)
-
     def kmm(i, n, t, ra, done):
         mm(i, n, T.qx, T.sx, 128 * t, T.qw1, T.sw1, ra, done)
 
-    PE.wait_ge(S.qx0, 1)
     PE.wait_ge(S.qw1, 1)
+    PE.wait_ge(S.qx0, 1)
     hmm(0, 128, 5, 6, S.mh0a, S.mh0b)
-    if hfirst:
-        PE.wait_ge(S.qx1, 1)
-        PE.wait_ge(S.qx2, 1)
-        h1mm()
     kmm(0, 256, 0, 0, S.mk0)
     PE.wait_ge(S.qx1, 1)
     kmm(1, 256, 1, 0, S.mk1)
     PE.wait_ge(S.qx2, 1)
     kmm(2, 256, 2, 0, S.mk2)
+    PE.wait_ge(S.qx3, 1)
     kmm(3, 128, 3, 0, S.mk3a)
     kmm(4, 128, 3, 128, S.mk3b)
-    if not hfirst:
-        h1mm()
-
-    def vh1():
-        V.wait_ge(S.mh1a, 1)
-        vrelu(hcols(128, 512, 0), 7, 384, 1, S.eh1)
-        vrelu(hcols(128, 512, 1), 7, 384, -1, S.eh1)
-        quant(S.eh1, 4, T.qh, T.sh, T.ht, 128, 512, S.qh1)
+    PE.wait_ge(S.eh0, 4)
+    hmm(128, 512, 7, 6, S.mh1a, S.mh1b)
 
     quant(S.lw1, 16, T.qw1, T.sw1, T.w1b, 0, 256, S.qw1)
     quant(S.lx0, 16, T.qx, T.sx, T.xb, 0, 128, S.qx0)
@@ -160,9 +154,8 @@ def rank_program(g, core, T, topo):
     vrelu(hcols(0, 128, 1), 5, 128, -1, S.eh0)
     quant(S.lx1, 16, T.qx, T.sx, T.xb, 128, 256, S.qx1)
     quant(S.eh0, 4, T.qh, T.sh, T.ht, 0, 128, S.qh0)
-    quant(S.lx2, 16, T.qx, T.sx, T.xb, 256, 512, S.qx2)
-    if hfirst:
-        vh1()
+    quant(S.lx2, 16, T.qx, T.sx, T.xb, 256, 384, S.qx2)
+    quant(S.lx2, 16, T.qx, T.sx, T.xb, 384, 512, S.qx3)
     V.wait_ge(S.mk2, 1)
     vrelu(kcols(0, 2), 2, 256, 1, S.et2)
     V.wait_ge(S.mk3a, 1)
@@ -171,21 +164,16 @@ def rank_program(g, core, T, topo):
     quant(S.ekp, 4, T.qk, T.sk, T.kt, 0, 256, S.qk0)
     vrelu(kcols(1, 3, 0), 3, 128, -1, S.ekm)
     quant(S.ekm, 5, T.qk, T.sk, T.kt, 256, 512, S.qk1)
-    if not hfirst:
-        vh1()
+    V.wait_ge(S.mh1a, 1)
+    vrelu(hcols(128, 512, 0), 7, 384, 1, S.eh1)
+    vrelu(hcols(128, 512, 1), 7, 384, -1, S.eh1)
+    quant(S.eh1, 4, T.qh, T.sh, T.ht, 128, 512, S.qh1)
     quant(S.le, 16, T.qe, T.se, T.eb, 0, 512, S.qe)
     quant(S.lw2, 16, T.qw2, T.sw2, T.w2b, 0, 128, S.qw2)
-
-    def ah1():
-        A.wait_ge(S.mh1b, 1)
-        arelu(hcols(128, 512, 2), 6, 384, 1, S.eh1)
-        arelu(hcols(128, 512, 3), 6, 384, -1, S.eh1)
 
     A.wait_ge(S.mh0b, 1)
     arelu(hcols(0, 128, 2), 6, 128, 1, S.eh0)
     arelu(hcols(0, 128, 3), 6, 128, -1, S.eh0)
-    if hfirst:
-        ah1()
     for t, m in ((0, S.mk0), (1, S.mk1)):
         A.wait_ge(m, 1)
         arelu(kcols(0, t), t, 256, 1, S.ekp)
@@ -195,51 +183,45 @@ def rank_program(g, core, T, topo):
     A.wait_ge(S.et2, 1)
     arelu(kcols(1, 2), 2, 256, -1, S.ekm)
     arelu(kcols(1, 3, 1), 4, 128, -1, S.ekm)
-    if not hfirst:
-        ah1()
+    A.wait_ge(S.mh1b, 1)
+    arelu(hcols(128, 512, 2), 6, 384, 1, S.eh1)
+    arelu(hcols(128, 512, 3), 6, 384, -1, S.eh1)
 
     sent = 0
-    for p, route in sends:
+    for p, route in routes[rank]:
         for e in PIECES[p][2]:
             g.wait_ge(S[e], 1)
         sent += _send(g, T, topo, route, 0, p)
     g.wait_ge(S.sent, sent)
 
-    def do_y():
-        PE.wait_ge(S.qw2, 1)
-        PE.wait_ge(S.eh0, 4)
-        for p in ("hc0", "hc1", "hs"):
-            PE.wait_ge(S["a" + p], arrive[p])
-        mm(5, 512, T.qw2, T.sw2, 0, T.rh, T.rhs, 0, S.my)
-        V.wait_ge(S.my, 1)
-        V.tensor_copy(T.yb[:], bank(5, 512)).then_inc(S.ey, 1)
-        SY.wait_ge(S.ey, 1)
-        SY.dma_start(T.y[:], T.yb[:]).then_inc(S.st, 16)
+    used = []
 
-    def do_z():
-        PE.wait_ge(S.qe, 1)
-        PE.wait_ge(S.ekm, 5)
-        PE.wait_ge(S.ekp, 4)
-        PE.wait_ge(S.et2, 1)
-        for pieces, blocks in ((("kc0", "ks"), (0, 2)), (("kc1",), (1, 3))):
-            for p in pieces:
+    def product(l, ls, la, r, rs, n, buf, col, out):
+        i = 2 * (len(used) % 4)
+        if len(used) > 3:
+            PE.wait_ge(S["e" + used[-4]], 2)
+        used.append(n)
+        m, m2, e = S["m" + n], S["n" + n], S["e" + n]
+        mm(i, 256, l, ls, la, r, rs, 0, m)
+        mm(i + 1, 256, l, ls, la, r, rs, 256, m2)
+        V.wait_ge(m, 1)
+        V.tensor_copy(buf[:, col:col + 256], bank(i, 256)).then_inc(e, 1)
+        A.wait_ge(m2, 1)
+        A.activation(buf[:, col + 256:col + 512], bank(i + 1, 256), ActivationFunctionType.Copy).then_inc(e, 1)
+        SY.wait_ge(e, 2)
+        SY.dma_start(out[:, col:col + 512], buf[:, col:col + 512]).then_inc(S.st, 16)
+
+    for e, n in ((S.qe, 1), (S.ekm, 5), (S.ekp, 4), (S.et2, 1), (S.eh1, 4)):
+        PE.wait_ge(e, n)
+    for pieces, blocks in ((("kc0", "ks", "ks0"), (0, 2)), (("kc1", "ks1"), (1, 3))):
+        for p in pieces:
+            if p in arrive:
                 PE.wait_ge(S["a" + p], arrive[p])
-            for i, b in enumerate(blocks):
-                m, e = S["mz%d" % b], S["ez%d" % b]
-                mm(1 + POS[b], 512, T.rk, T.rks, 128 * POS[b], T.qe, T.se, 0, m)
-                (V, A)[i].wait_ge(m, 1)
-                dst = T.zb[:, 512 * b:512 * b + 512]
-                if i == 0:
-                    V.tensor_copy(dst, bank(1 + POS[b], 512)).then_inc(e, 1)
-                else:
-                    A.activation(dst, bank(1 + POS[b], 512), ActivationFunctionType.Copy).then_inc(e, 1)
-                SY.wait_ge(e, 1)
-                SY.dma_start(T.z[:, 512 * b:512 * b + 512], dst).then_inc(S.st, 16)
-
-    if [len(route) for p, route in routes[(rank + 1) % len(T.cores)] if p == "ks"][0] > 2:
-        do_y()
-        do_z()
-    else:
-        do_z()
-        do_y()
+        for b in blocks:
+            product(T.rk, T.rks, 128 * POS[b], T.qe, T.se, "z%d" % b, T.zb, 512 * b, T.z)
+    PE.wait_ge(S.qw2, 1)
+    for p in arrive:
+        if p[0] == "h":
+            PE.wait_ge(S["a" + p], arrive[p])
+    product(T.qw2, T.sw2, 0, T.rh, T.rhs, "y", T.yb, 0, T.y)
     SY.wait_ge(S.st, 80)

@@ -16,52 +16,65 @@ SCRATCH = {
     "yb": ("sbuf", [128, 512], F32), "zb": ("sbuf", [128, 2048], F32),
     "ps": ("psum", [128, 4096], F32),
 }
-PIECES = {"hc0": (0, 128, ["qh0"]), "hc1": (128, 512, ["qh1"]), "hc2": (128, 384, ["qh1"]), "hc3": (384, 512, ["qh1"]),
-          "hs": (0, 512, ["qh0", "qh1"]), "hs0": (0, 128, ["qh0"]), "hs1": (128, 512, ["qh1"]),
-          "kc0": (0, 256, ["qk0"]), "kc1": (256, 512, ["qk1"]), "ks": (0, 512, ["qk0", "qk1"]),
-          "ks0": (0, 256, ["qk0"]), "ks1": (256, 512, ["qk1"])}
-POS = {0: 0, 2: 1, 1: 2, 3: 3}
 C = 0.043
-SEMAPHORES = (["lx0", "lx1", "lx2", "lw1", "lw2", "le", "qx0", "qx1", "qx2", "qx3", "qw1", "qw2", "qe"]
-              + ["mh0a", "mh0b", "mk0", "mk1", "mk2", "mk3a", "mk3b", "mh1a", "mh1b"]
-              + ["eh0", "eh1", "ekp", "ekm", "et2", "qh0", "qh1", "qk0", "qk1"]
-              + [a + b for a in ("mz", "nz", "ez") for b in "0123"] + ["my", "ny", "ey", "st", "sent"]
-              + ["a" + p for p in PIECES])
+NAMES = ["%s%s%d%d" % (t, k, a, b) for t in "hk" for k in "cs" for a in range(4) for b in range(a + 1, 5)]
+MADE = {"h": {"qhA": (0, 1), "qhB": (1, 2), "qhC": (2, 4)}, "k": {"qk0": (0, 1), "qk1": (1, 2), "qk2": (2, 4)}}
+PLAN = {
+    "far_k": "hs01:N hc01:O kc01:N ks02:O kc12:O kc23:N kc34:O ks24:N hs14:O hc13:D hc34:O",
+    "far_h": "hs01:O hc01:N kc02:D ks04:D kc24:D hc12:N hs14:O hc23:N hc34:O",
+    "cross_k": "hs01:O hc01:O kc02:D ks04:D kc24:D hc12:O hs14:O hc24:O",
+    "cross_h": "hs01:N hc01:N kc02:D ks04:D kc24:D hc12:N hs14:N hc24:N",
+    "turn": "hs01:O hc01:O kc02:D ks04:D kc24:D hc12:N hs14:O hc24:N",
+    "plain": "hs01:O hc01:O kc02:D ks04:D kc24:D hc12:O hs14:O hc24:O",
+}
+ORDER = ["z0", "z1", "z2", "z3", "y"]
+HALF = ("z0", "y")
+PEO = "hA k00 k10 k20 k30 k01 k11 k21 k31 hB hC"
+VO = "wa x0 wb hA x1 qA x2 x3 k30+ k30- q0 q1 k31+ k31- hB q2 hC qB e0 qC e1 w2"
+VO_FAR_K = "wa x0 wb hA qA x1 x2 x3 k30+ k30- q0 q1 k31+ k31- hB q2 hC qB e0 qC e1 w2"
+AO = "hA k00+ k00- k10+ k10- k20+ k20- k01+ k01- k11+ k11- k21+ k21- hB hC"
+HB = {"A": (0, 128, 4, 5), "B": (128, 256, 4, 5), "C": (256, 512, 2, 3)}
+KB = {(0, 0): 0, (1, 0): 1, (2, 0): 2, (3, 0): 3, (0, 1): 6, (1, 1): 7, (2, 1): 0, (3, 1): 1}
+SEMAPHORES = (["lx0", "lx1", "lx2", "lx3", "lwa", "lwb", "lw2", "le", "qx0", "qx1", "qx2", "qx3", "qwa", "qwb", "qw2", "qe0", "qe1"]
+              + ["qhA", "qhB", "qhC", "qk0", "qk1", "qk2", "ehA", "ehB", "ehC"]
+              + ["m" + a + b for a in "ABC" for b in "01"]
+              + ["mk%d%d" % tp for tp in KB] + ["ek%d%s" % (p, s) for p in (0, 1) for s in "pm"]
+              + [a + b for a in ("mz", "nz", "ez", "fz") for b in "0123"] + ["my", "ny", "ey", "fy", "st", "sent"]
+              + ["a" + p for p in NAMES])
 
 
 def _mask(topo, route, i, p):
     m, out = topo.mask(route[i], route[i + 1]), topo.mask(route[i], route[-1])
-    if p in ("hc0", "hs0"):
-        return m & out
-    if p in ("hc3", "hs") and m != out:
-        return m & ~out
+    if i == 0 and m != out and p[0] == "h":
+        return m & out if p == "hs01" else m & ~out
     return m
+
+
+def _kind(T, topo, r):
+    n = len(T.cores)
+    src, hd, kd = T.cores[r], T.cores[(r + 1) % n], T.cores[(r - 1) % n]
+    for k, d in (("h", hd), ("k", kd)):
+        if not topo.may_write(src, d):
+            return "far_" + k
+        if not topo.same_plane(topo.chip(src), topo.chip(d)):
+            return "cross_" + k
+    return "plain" if topo.die(T.cores[(r + 2) % n]) == topo.die(hd) else "turn"
 
 
 def _routes(T, topo):
     n, out = len(T.cores), []
     for r in range(n):
         src, hd, kd = T.cores[r], T.cores[(r + 1) % n], T.cores[(r - 1) % n]
-        far = [d for d in (hd, kd) if not topo.may_write(src, d)]
         a, b = [[c for c in range(64) if c not in T.cores and topo.chip(c) == topo.chip(src)
-                 and (topo.die(c) == topo.die(src)) == same and all(topo.may_write(c, d) for d in far + [hd])][0]
+                 and (topo.die(c) == topo.die(src)) == same and all(topo.may_write(c, d) for d in (hd, kd))][0]
                 for same in (True, False)]
-        direct, other, near = [src, hd], [src, b, hd], [src, a, hd]
-        if far == [kd]:
-            out.append([("hs0", near), ("hc0", other), ("kc0", [src, a, kd]), ("ks0", [src, a, kd]), ("kc1", [src, b, kd]),
-                        ("ks1", [src, b, kd]), ("hc3", other), ("hs1", other), ("hc2", direct)])
-        elif far == [hd]:
-            out.append([("hs0", other), ("hc0", near), ("kc0", [src, kd]), ("ks", [src, kd]), ("kc1", [src, kd]),
-                        ("hc1", near), ("hs1", other)])
-        else:
-            out.append([("hc0", other), ("kc0", [src, kd]), ("ks", [src, kd]), ("kc1", [src, kd]),
-                        ("hc3", other), ("hs", other), ("hc2", direct)])
+        way = {"D": [], "N": [a], "O": [b]}
+        out.append([(w[:4], [src] + way[w[5]] + [hd if w[0] == "h" else kd]) for w in PLAN[_kind(T, topo, r)].split()])
     return out
 
 
 def _send(g, T, topo, route, i, p):
-    a, b, _ = PIECES[p]
-    t = p[0]
+    a, b, t = 128 * int(p[2]), 128 * int(p[3]), p[0]
     if p[1] == "c":
         s = T[("r" if i else "q") + t][:, a:b].bitcast(dt.uint8)
         d = T["r" + t][:, a:b].bitcast(dt.uint8)
@@ -95,133 +108,140 @@ def rank_program(g, core, T, topo):
     S = T.sem
     V, A, PE, SY = g.vector, g.scalar, g.tensor, g.sync
 
-    SY.dma_start(T.w1b[:], T.w1[:]).then_inc(S.lw1, 16)
-    for a, b, e in ((0, 512, S.lx0), (512, 1024, S.lx1), (1024, 2048, S.lx2)):
-        SY.dma_start(T.xb[:, a:b], T.x[:, a:b]).then_inc(e, 16)
+    for name, b, f, i in (("lwa", T.w1b, T.w1, 0), ("lx0", T.xb, T.x, 0), ("lwb", T.w1b, T.w1, 1),
+                          ("lx1", T.xb, T.x, 1), ("lx2", T.xb, T.x, 2), ("lx3", T.xb, T.x, 3)):
+        SY.dma_start(b[:, 512 * i:512 * i + 512], f[:, 512 * i:512 * i + 512]).then_inc(S[name], 16)
     SY.wait_ge(S.lx0, 16)
     SY.dma_start(T.eb[:], T.e[:]).then_inc(S.le, 16)
     SY.dma_start(T.w2b[:], T.w2[:]).then_inc(S.lw2, 16)
-
-    def quant(sem, n, q, s, src, a, b, done):
-        V.wait_ge(sem, n)
-        V.quantize_mx(q[:, a:b], s[:, a:b], src[:, 4 * a:4 * b]).then_inc(done, 1)
 
     def bank(i, n):
         return T.ps[:, 512 * i:512 * i + n]
 
     def mm(i, n, l, ls, la, r, rs, ra, done):
         PE.matmul_mx(bank(i, n), l[:, la:la + 128], ls[:, la:la + 128], r[:, ra:ra + n], rs[:, ra:ra + n],
-                     True, True).then_inc(done, 1)
+                     True, True).then_inc(S[done], 1)
 
-    def vrelu(out, i, n, sign, done):
-        V.tensor_scalar(out, bank(i, n), sign * C, 0.0, AluOpType.mult, AluOpType.max).then_inc(done, 1)
+    def relu(q, out, i, n, sign, done):
+        if q is V:
+            V.tensor_scalar(out, bank(i, n), sign * C, 0.0, AluOpType.mult, AluOpType.max).then_inc(S[done], 1)
+        else:
+            A.activation(out, bank(i, n), ActivationFunctionType.Relu, scale=sign * C).then_inc(S[done], 1)
 
-    def arelu(out, i, n, sign, done):
-        A.activation(out, bank(i, n), ActivationFunctionType.Relu, scale=sign * C).then_inc(done, 1)
+    def hpart(q, n, i):
+        a, b = HB[n][:2]
+        q.wait_ge(S["m%s%d" % (n, i)], 1)
+        for k, sign in ((0, 1), (1, -1)):
+            relu(q, T.ht[:, 4 * a + 2 * i + k:4 * b:4], HB[n][2 + i], b - a, sign, "eh" + n)
 
-    def hcols(a, b, k):
-        return T.ht[:, 4 * a + k:4 * b:4]
+    def kpart(q, o):
+        t, p, neg = int(o[1]), int(o[2]), o[3] == "-"
+        q.wait_ge(S["mk%d%d" % (t, p)], 1)
+        a = 512 * (2 * p + neg)
+        relu(q, T.kt[:, a + t:a + 512:4], KB[t, p], 128, -1 if neg else 1, "ek%d%s" % (p, "m" if neg else "p"))
 
-    def kcols(half, t, i=None):
-        a = 1024 * half + (0 if i is None else 512 * i)
-        return T.kt[:, a + t:a + (1024 if i is None else 512):4]
+    def quant(waits, q, s, src, a, b, done):
+        for w, n in waits:
+            V.wait_ge(S[w], n)
+        V.quantize_mx(q[:, a:b], s[:, a:b], src[:, 4 * a:4 * b]).then_inc(S[done], 1)
 
-    def hmm(a, b, ba, bb, sa, sb):
-        mm(ba, b - a, T.qw1, T.sw1, 0, T.qx, T.sx, a, sa)
-        mm(bb, b - a, T.qw1, T.sw1, 128, T.qx, T.sx, a, sb)
+    PE.wait_ge(S.qwa, 1)
+    for o in PEO.split():
+        if o[0] == "k":
+            t, p = int(o[1]), int(o[2])
+            PE.wait_ge(S["qx%d" % t], 1)
+            if o == "k21":
+                PE.wait_ge(S.ek0p, 4)
+                PE.wait_ge(S.ek0m, 4)
+            mm(KB[t, p], 128, T.qx, T.sx, 128 * t, T.qw1, T.sw1, 128 * p, "mk%d%d" % (t, p))
+        else:
+            n = o[1]
+            a, b = HB[n][:2]
+            PE.wait_ge(S["qx%d" % (b // 128 - 1)], 1)
+            if n == "B":
+                PE.wait_ge(S.ehA, 4)
+            for i, w in ((0, S.qwa), (1, S.qwb)):
+                PE.wait_ge(w, 1)
+                mm(HB[n][2 + i], b - a, T.qw1, T.sw1, 128 * i, T.qx, T.sx, a, "m%s%d" % (n, i))
 
-    def kmm(i, n, t, ra, done):
-        mm(i, n, T.qx, T.sx, 128 * t, T.qw1, T.sw1, ra, done)
+    for o in (VO_FAR_K if _kind(T, topo, rank) == "far_k" else VO).split():
+        if o in ("wa", "wb"):
+            a = 128 * "ab".index(o[1])
+            quant([("l" + o, 16)], T.qw1, T.sw1, T.w1b, a, a + 128, "q" + o)
+        elif o[0] == "x":
+            t = int(o[1])
+            quant([("lx%d" % t, 16)], T.qx, T.sx, T.xb, 128 * t, 128 * t + 128, "qx%d" % t)
+        elif o[0] == "h":
+            hpart(V, o[1], 0)
+        elif o[0] == "k":
+            kpart(V, o)
+        elif o == "q0":
+            quant([("ek0p", 4)], T.qk, T.sk, T.kt, 0, 128, "qk0")
+        elif o == "q1":
+            quant([("ek0m", 4)], T.qk, T.sk, T.kt, 128, 256, "qk1")
+        elif o == "q2":
+            quant([("ek1p", 4), ("ek1m", 4)], T.qk, T.sk, T.kt, 256, 512, "qk2")
+        elif o[0] == "q":
+            quant([("eh" + o[1], 4)], T.qh, T.sh, T.ht, HB[o[1]][0], HB[o[1]][1], "qh" + o[1])
+        elif o[0] == "e":
+            a = 256 * int(o[1])
+            quant([("le", 16)], T.qe, T.se, T.eb, a, a + 256, "q" + o)
+        else:
+            quant([("lw2", 16)], T.qw2, T.sw2, T.w2b, 0, 128, "qw2")
 
-    PE.wait_ge(S.qw1, 1)
-    PE.wait_ge(S.qx0, 1)
-    hmm(0, 128, 5, 6, S.mh0a, S.mh0b)
-    kmm(0, 256, 0, 0, S.mk0)
-    PE.wait_ge(S.qx1, 1)
-    kmm(1, 256, 1, 0, S.mk1)
-    PE.wait_ge(S.qx2, 1)
-    kmm(2, 256, 2, 0, S.mk2)
-    PE.wait_ge(S.qx3, 1)
-    kmm(3, 128, 3, 0, S.mk3a)
-    kmm(4, 128, 3, 128, S.mk3b)
-    PE.wait_ge(S.eh0, 4)
-    hmm(128, 512, 7, 6, S.mh1a, S.mh1b)
-
-    quant(S.lw1, 16, T.qw1, T.sw1, T.w1b, 0, 256, S.qw1)
-    quant(S.lx0, 16, T.qx, T.sx, T.xb, 0, 128, S.qx0)
-    V.wait_ge(S.mh0a, 1)
-    vrelu(hcols(0, 128, 0), 5, 128, 1, S.eh0)
-    vrelu(hcols(0, 128, 1), 5, 128, -1, S.eh0)
-    quant(S.lx1, 16, T.qx, T.sx, T.xb, 128, 256, S.qx1)
-    quant(S.eh0, 4, T.qh, T.sh, T.ht, 0, 128, S.qh0)
-    quant(S.lx2, 16, T.qx, T.sx, T.xb, 256, 384, S.qx2)
-    quant(S.lx2, 16, T.qx, T.sx, T.xb, 384, 512, S.qx3)
-    V.wait_ge(S.mk2, 1)
-    vrelu(kcols(0, 2), 2, 256, 1, S.et2)
-    V.wait_ge(S.mk3a, 1)
-    vrelu(kcols(0, 3, 0), 3, 128, 1, S.ekp)
-    V.wait_ge(S.et2, 1)
-    quant(S.ekp, 4, T.qk, T.sk, T.kt, 0, 256, S.qk0)
-    vrelu(kcols(1, 3, 0), 3, 128, -1, S.ekm)
-    quant(S.ekm, 5, T.qk, T.sk, T.kt, 256, 512, S.qk1)
-    V.wait_ge(S.mh1a, 1)
-    vrelu(hcols(128, 512, 0), 7, 384, 1, S.eh1)
-    vrelu(hcols(128, 512, 1), 7, 384, -1, S.eh1)
-    quant(S.eh1, 4, T.qh, T.sh, T.ht, 128, 512, S.qh1)
-    quant(S.le, 16, T.qe, T.se, T.eb, 0, 512, S.qe)
-    quant(S.lw2, 16, T.qw2, T.sw2, T.w2b, 0, 128, S.qw2)
-
-    A.wait_ge(S.mh0b, 1)
-    arelu(hcols(0, 128, 2), 6, 128, 1, S.eh0)
-    arelu(hcols(0, 128, 3), 6, 128, -1, S.eh0)
-    for t, m in ((0, S.mk0), (1, S.mk1)):
-        A.wait_ge(m, 1)
-        arelu(kcols(0, t), t, 256, 1, S.ekp)
-        arelu(kcols(1, t), t, 256, -1, S.ekm)
-    A.wait_ge(S.mk3b, 1)
-    arelu(kcols(0, 3, 1), 4, 128, 1, S.ekp)
-    A.wait_ge(S.et2, 1)
-    arelu(kcols(1, 2), 2, 256, -1, S.ekm)
-    arelu(kcols(1, 3, 1), 4, 128, -1, S.ekm)
-    A.wait_ge(S.mh1b, 1)
-    arelu(hcols(128, 512, 2), 6, 384, 1, S.eh1)
-    arelu(hcols(128, 512, 3), 6, 384, -1, S.eh1)
+    for o in AO.split():
+        if o[0] == "h":
+            hpart(A, o[1], 1)
+        else:
+            kpart(A, o)
 
     sent = 0
     for p, route in routes[rank]:
-        for e in PIECES[p][2]:
-            g.wait_ge(S[e], 1)
+        for e, (a, b) in MADE[p[0]].items():
+            if a < int(p[3]) and b > int(p[2]):
+                g.wait_ge(S[e], 1)
         sent += _send(g, T, topo, route, 0, p)
     g.wait_ge(S.sent, sent)
 
-    used = []
+    for e, n in (("ek1p", 4), ("ek1m", 4), ("ehB", 4), ("ehC", 4)):
+        PE.wait_ge(S[e], n)
+    seen = []
 
-    def product(l, ls, la, r, rs, n, buf, col, out):
-        i = 2 * (len(used) % 4)
-        if len(used) > 3:
-            PE.wait_ge(S["e" + used[-4]], 2)
-        used.append(n)
-        m, m2, e = S["m" + n], S["n" + n], S["e" + n]
-        mm(i, 256, l, ls, la, r, rs, 0, m)
-        mm(i + 1, 256, l, ls, la, r, rs, 256, m2)
-        V.wait_ge(m, 1)
-        V.tensor_copy(buf[:, col:col + 256], bank(i, 256)).then_inc(e, 1)
-        A.wait_ge(m2, 1)
-        A.activation(buf[:, col + 256:col + 512], bank(i + 1, 256), ActivationFunctionType.Copy).then_inc(e, 1)
-        SY.wait_ge(e, 2)
-        SY.dma_start(out[:, col:col + 512], buf[:, col:col + 512]).then_inc(S.st, 16)
-
-    for e, n in ((S.qe, 1), (S.ekm, 5), (S.ekp, 4), (S.et2, 1), (S.eh1, 4)):
-        PE.wait_ge(e, n)
-    for pieces, blocks in ((("kc0", "ks", "ks0"), (0, 2)), (("kc1", "ks1"), (1, 3))):
-        for p in pieces:
-            if p in arrive:
+    def arrived(t, a, b):
+        for p in sorted(arrive, key=lambda p: (int(p[2]), p)):
+            if p[0] == t and int(p[2]) < b and int(p[3]) > a and p not in seen:
                 PE.wait_ge(S["a" + p], arrive[p])
-        for b in blocks:
-            product(T.rk, T.rks, 128 * POS[b], T.qe, T.se, "z%d" % b, T.zb, 512 * b, T.z)
-    PE.wait_ge(S.qw2, 1)
-    for p in arrive:
-        if p[0] == "h":
-            PE.wait_ge(S["a" + p], arrive[p])
-    product(T.qw2, T.sw2, 0, T.rh, T.rhs, "y", T.yb, 0, T.y)
-    SY.wait_ge(S.st, 80)
+                seen.append(p)
+
+    stored = 0
+    for j, n in enumerate(ORDER):
+        i = 2 * (j % 4)
+        if j > 3:
+            PE.wait_ge(S["e" + ORDER[j - 4]], 1)
+            PE.wait_ge(S["f" + ORDER[j - 4]], 1)
+        if n == "y":
+            PE.wait_ge(S.qw2, 1)
+            l, ls, la, r, rs, buf, col, out = T.qw2, T.sw2, 0, T.rh, T.rhs, T.yb, 0, T.y
+        else:
+            b = int(n[1])
+            l, ls, la, r, rs, buf, col, out = T.rk, T.rks, 128 * b, T.qe, T.se, T.zb, 512 * b, T.z
+            arrived("k", b, b + 1)
+        for half, m in ((0, "m" + n), (1, "n" + n)):
+            if n == "y":
+                arrived("h", 2 * half, 2 * half + 2)
+            else:
+                PE.wait_ge(S["qe%d" % half], 1)
+            mm(i + half, 256, l, ls, la, r, rs, 256 * half, m)
+        V.wait_ge(S["m" + n], 1)
+        V.tensor_copy(buf[:, col:col + 256], bank(i, 256)).then_inc(S["e" + n], 1)
+        A.wait_ge(S["n" + n], 1)
+        A.activation(buf[:, col + 256:col + 512], bank(i + 1, 256), ActivationFunctionType.Copy).then_inc(S["f" + n], 1)
+        SY.wait_ge(S["e" + n], 1)
+        if n in HALF:
+            SY.dma_start(out[:, col:col + 256], buf[:, col:col + 256]).then_inc(S.st, 16)
+            stored += 16
+        SY.wait_ge(S["f" + n], 1)
+        a = col + (256 if n in HALF else 0)
+        SY.dma_start(out[:, a:col + 512], buf[:, a:col + 512]).then_inc(S.st, 16)
+        stored += 16
+    SY.wait_ge(S.st, stored)

from concourse.mybir import dt, AluOpType, ActivationFunctionType

CODES, BF, F32, U8 = "float8_e4m3fn_x4", "bfloat16", "float32", "uint8"
SCRATCH = {
    "xb": ("sbuf", [128, 2048], BF), "w1b": ("sbuf", [128, 1024], BF),
    "w2b": ("sbuf", [128, 512], BF), "eb": ("sbuf", [128, 2048], BF),
    "qx": ("sbuf", [128, 512], CODES), "sx": ("sbuf", [128, 512], U8),
    "qw1": ("sbuf", [128, 256], CODES), "sw1": ("sbuf", [128, 256], U8),
    "qw2": ("sbuf", [128, 128], CODES), "sw2": ("sbuf", [128, 128], U8),
    "qe": ("sbuf", [128, 512], CODES), "se": ("sbuf", [128, 512], U8),
    "ht": ("sbuf", [128, 2048], BF), "kt": ("sbuf", [128, 2048], BF),
    "qh": ("sbuf", [128, 512], CODES), "sh": ("sbuf", [128, 512], U8),
    "qk": ("sbuf", [128, 512], CODES), "sk": ("sbuf", [128, 512], U8),
    "rh": ("sbuf", [128, 512], CODES), "rhs": ("sbuf", [128, 512], U8),
    "rk": ("sbuf", [128, 512], CODES), "rks": ("sbuf", [128, 512], U8),
    "yb": ("sbuf", [128, 512], F32), "zb": ("sbuf", [128, 2048], F32),
    "ps": ("psum", [128, 4096], F32),
}
C = 0.043
NAMES = ["%s%s%d%d" % (t, k, a, b) for t in "hk" for k in "cs" for a in range(4) for b in range(a + 1, 5)]
MADE = {"h": {"qhA": (0, 1), "qhB": (1, 2), "qhC": (2, 4)}, "k": {"qk0": (0, 1), "qk1": (1, 2), "qk2": (2, 4)}}
PLAN = {
    "far_k": "hs01:N hc01:O kc01:N ks02:O kc12:O kc23:N kc34:O ks24:N hs14:O hc13:D hc34:O",
    "far_h": "hs01:O hc01:N kc02:D ks04:D kc24:D hc12:N hs14:O hc23:N hc34:O",
    "cross_k": "hs01:O hc01:O kc02:D ks04:D kc24:D hc12:O hs14:O hc24:O",
    "cross_h": "hs01:N hc01:N kc02:D ks04:D kc24:D hc12:N hs14:N hc24:N",
    "turn": "hs01:O hc01:O kc02:D ks04:D kc24:D hc12:N hs14:O hc24:N",
    "plain": "hs01:O hc01:O kc02:D ks04:D kc24:D hc12:O hs14:O hc24:O",
}
ORDER = ["z0", "z1", "z2", "z3", "y"]
HALF = ("z0", "y")
PEO = "hA k00 k10 k20 k30 k01 k11 k21 k31 hB hC"
VO = "wa x0 wb hA x1 qA x2 x3 k30+ k30- q0 q1 k31+ k31- hB q2 hC qB e0 qC e1 w2"
VO_FAR_K = "wa x0 wb hA qA x1 x2 x3 k30+ k30- q0 q1 k31+ k31- hB q2 hC qB e0 qC e1 w2"
AO = "hA k00+ k00- k10+ k10- k20+ k20- k01+ k01- k11+ k11- k21+ k21- hB hC"
HB = {"A": (0, 128, 4, 5), "B": (128, 256, 4, 5), "C": (256, 512, 2, 3)}
KB = {(0, 0): 0, (1, 0): 1, (2, 0): 2, (3, 0): 3, (0, 1): 6, (1, 1): 7, (2, 1): 0, (3, 1): 1}
SEMAPHORES = (["lx0", "lx1", "lx2", "lx3", "lwa", "lwb", "lw2", "le", "qx0", "qx1", "qx2", "qx3", "qwa", "qwb", "qw2", "qe0", "qe1"]
              + ["qhA", "qhB", "qhC", "qk0", "qk1", "qk2", "ehA", "ehB", "ehC"]
              + ["m" + a + b for a in "ABC" for b in "01"]
              + ["mk%d%d" % tp for tp in KB] + ["ek%d%s" % (p, s) for p in (0, 1) for s in "pm"]
              + [a + b for a in ("mz", "nz", "ez", "fz") for b in "0123"] + ["my", "ny", "ey", "fy", "st", "sent"]
              + ["a" + p for p in NAMES])


def _mask(topo, route, i, p):
    m, out = topo.mask(route[i], route[i + 1]), topo.mask(route[i], route[-1])
    if i == 0 and m != out and p[0] == "h":
        return m & out if p == "hs01" else m & ~out
    return m


def _kind(T, topo, r):
    n = len(T.cores)
    src, hd, kd = T.cores[r], T.cores[(r + 1) % n], T.cores[(r - 1) % n]
    for k, d in (("h", hd), ("k", kd)):
        if not topo.may_write(src, d):
            return "far_" + k
        if not topo.same_plane(topo.chip(src), topo.chip(d)):
            return "cross_" + k
    return "plain" if topo.die(T.cores[(r + 2) % n]) == topo.die(hd) else "turn"


def _routes(T, topo):
    n, out = len(T.cores), []
    for r in range(n):
        src, hd, kd = T.cores[r], T.cores[(r + 1) % n], T.cores[(r - 1) % n]
        a, b = [[c for c in range(64) if c not in T.cores and topo.chip(c) == topo.chip(src)
                 and (topo.die(c) == topo.die(src)) == same and all(topo.may_write(c, d) for d in (hd, kd))][0]
                for same in (True, False)]
        way = {"D": [], "N": [a], "O": [b]}
        out.append([(w[:4], [src] + way[w[5]] + [hd if w[0] == "h" else kd]) for w in PLAN[_kind(T, topo, r)].split()])
    return out


def _send(g, T, topo, route, i, p):
    a, b, t = 128 * int(p[2]), 128 * int(p[3]), p[0]
    if p[1] == "c":
        s = T[("r" if i else "q") + t][:, a:b].bitcast(dt.uint8)
        d = T["r" + t][:, a:b].bitcast(dt.uint8)
    else:
        s = T["r" + t + "s" if i else "s" + t][:, a:b]
        d = T["r" + t + "s"][:, a:b]
    rid, pid, _ = topo.addr(route[i + 1])
    m = _mask(topo, route, i, p)
    g.remote_dma(d, s, T.sem["a" + p], T.sem.sent, pid, rid, m)
    return m.bit_count()


def rank_program(g, core, T, topo):
    routes = _routes(T, topo)
    arrive = {}
    for sends in routes:
        for p, route in sends:
            if core in route[1:]:
                arrive[p] = _mask(topo, route, route.index(core) - 1, p).bit_count()
    rank = T.rank_of(core)
    if rank is None:
        sent = 0
        for sends in routes:
            for p, route in sends:
                if core in route:
                    g.wait_ge(T.sem["a" + p], arrive[p])
                    sent += _send(g, T, topo, route, 1, p)
        if sent:
            g.wait_ge(T.sem.sent, sent)
        return
    S = T.sem
    V, A, PE, SY = g.vector, g.scalar, g.tensor, g.sync

    for name, b, f, i in (("lwa", T.w1b, T.w1, 0), ("lx0", T.xb, T.x, 0), ("lwb", T.w1b, T.w1, 1),
                          ("lx1", T.xb, T.x, 1), ("lx2", T.xb, T.x, 2), ("lx3", T.xb, T.x, 3)):
        SY.dma_start(b[:, 512 * i:512 * i + 512], f[:, 512 * i:512 * i + 512]).then_inc(S[name], 16)
    SY.wait_ge(S.lx0, 16)
    SY.dma_start(T.eb[:], T.e[:]).then_inc(S.le, 16)
    SY.dma_start(T.w2b[:], T.w2[:]).then_inc(S.lw2, 16)

    def bank(i, n):
        return T.ps[:, 512 * i:512 * i + n]

    def mm(i, n, l, ls, la, r, rs, ra, done):
        PE.matmul_mx(bank(i, n), l[:, la:la + 128], ls[:, la:la + 128], r[:, ra:ra + n], rs[:, ra:ra + n],
                     True, True).then_inc(S[done], 1)

    def relu(q, out, i, n, sign, done):
        if q is V:
            V.tensor_scalar(out, bank(i, n), sign * C, 0.0, AluOpType.mult, AluOpType.max).then_inc(S[done], 1)
        else:
            A.activation(out, bank(i, n), ActivationFunctionType.Relu, scale=sign * C).then_inc(S[done], 1)

    def hpart(q, n, i):
        a, b = HB[n][:2]
        q.wait_ge(S["m%s%d" % (n, i)], 1)
        for k, sign in ((0, 1), (1, -1)):
            relu(q, T.ht[:, 4 * a + 2 * i + k:4 * b:4], HB[n][2 + i], b - a, sign, "eh" + n)

    def kpart(q, o):
        t, p, neg = int(o[1]), int(o[2]), o[3] == "-"
        q.wait_ge(S["mk%d%d" % (t, p)], 1)
        a = 512 * (2 * p + neg)
        relu(q, T.kt[:, a + t:a + 512:4], KB[t, p], 128, -1 if neg else 1, "ek%d%s" % (p, "m" if neg else "p"))

    def quant(waits, q, s, src, a, b, done):
        for w, n in waits:
            V.wait_ge(S[w], n)
        V.quantize_mx(q[:, a:b], s[:, a:b], src[:, 4 * a:4 * b]).then_inc(S[done], 1)

    PE.wait_ge(S.qwa, 1)
    for o in PEO.split():
        if o[0] == "k":
            t, p = int(o[1]), int(o[2])
            PE.wait_ge(S["qx%d" % t], 1)
            if o == "k21":
                PE.wait_ge(S.ek0p, 4)
                PE.wait_ge(S.ek0m, 4)
            mm(KB[t, p], 128, T.qx, T.sx, 128 * t, T.qw1, T.sw1, 128 * p, "mk%d%d" % (t, p))
        else:
            n = o[1]
            a, b = HB[n][:2]
            PE.wait_ge(S["qx%d" % (b // 128 - 1)], 1)
            if n == "B":
                PE.wait_ge(S.ehA, 4)
            for i, w in ((0, S.qwa), (1, S.qwb)):
                PE.wait_ge(w, 1)
                mm(HB[n][2 + i], b - a, T.qw1, T.sw1, 128 * i, T.qx, T.sx, a, "m%s%d" % (n, i))

    for o in (VO_FAR_K if _kind(T, topo, rank) == "far_k" else VO).split():
        if o in ("wa", "wb"):
            a = 128 * "ab".index(o[1])
            quant([("l" + o, 16)], T.qw1, T.sw1, T.w1b, a, a + 128, "q" + o)
        elif o[0] == "x":
            t = int(o[1])
            quant([("lx%d" % t, 16)], T.qx, T.sx, T.xb, 128 * t, 128 * t + 128, "qx%d" % t)
        elif o[0] == "h":
            hpart(V, o[1], 0)
        elif o[0] == "k":
            kpart(V, o)
        elif o == "q0":
            quant([("ek0p", 4)], T.qk, T.sk, T.kt, 0, 128, "qk0")
        elif o == "q1":
            quant([("ek0m", 4)], T.qk, T.sk, T.kt, 128, 256, "qk1")
        elif o == "q2":
            quant([("ek1p", 4), ("ek1m", 4)], T.qk, T.sk, T.kt, 256, 512, "qk2")
        elif o[0] == "q":
            quant([("eh" + o[1], 4)], T.qh, T.sh, T.ht, HB[o[1]][0], HB[o[1]][1], "qh" + o[1])
        elif o[0] == "e":
            a = 256 * int(o[1])
            quant([("le", 16)], T.qe, T.se, T.eb, a, a + 256, "q" + o)
        else:
            quant([("lw2", 16)], T.qw2, T.sw2, T.w2b, 0, 128, "qw2")

    for o in AO.split():
        if o[0] == "h":
            hpart(A, o[1], 1)
        else:
            kpart(A, o)

    sent = 0
    for p, route in routes[rank]:
        for e, (a, b) in MADE[p[0]].items():
            if a < int(p[3]) and b > int(p[2]):
                g.wait_ge(S[e], 1)
        sent += _send(g, T, topo, route, 0, p)
    g.wait_ge(S.sent, sent)

    for e, n in (("ek1p", 4), ("ek1m", 4), ("ehB", 4), ("ehC", 4)):
        PE.wait_ge(S[e], n)
    seen = []

    def arrived(t, a, b):
        for p in sorted(arrive, key=lambda p: (int(p[2]), p)):
            if p[0] == t and int(p[2]) < b and int(p[3]) > a and p not in seen:
                PE.wait_ge(S["a" + p], arrive[p])
                seen.append(p)

    stored = 0
    for j, n in enumerate(ORDER):
        i = 2 * (j % 4)
        if j > 3:
            PE.wait_ge(S["e" + ORDER[j - 4]], 1)
            PE.wait_ge(S["f" + ORDER[j - 4]], 1)
        if n == "y":
            PE.wait_ge(S.qw2, 1)
            l, ls, la, r, rs, buf, col, out = T.qw2, T.sw2, 0, T.rh, T.rhs, T.yb, 0, T.y
        else:
            b = int(n[1])
            l, ls, la, r, rs, buf, col, out = T.rk, T.rks, 128 * b, T.qe, T.se, T.zb, 512 * b, T.z
            arrived("k", b, b + 1)
        for half, m in ((0, "m" + n), (1, "n" + n)):
            if n == "y":
                arrived("h", 2 * half, 2 * half + 2)
            else:
                PE.wait_ge(S["qe%d" % half], 1)
            mm(i + half, 256, l, ls, la, r, rs, 256 * half, m)
        V.wait_ge(S["m" + n], 1)
        V.tensor_copy(buf[:, col:col + 256], bank(i, 256)).then_inc(S["e" + n], 1)
        A.wait_ge(S["n" + n], 1)
        A.activation(buf[:, col + 256:col + 512], bank(i + 1, 256), ActivationFunctionType.Copy).then_inc(S["f" + n], 1)
        SY.wait_ge(S["e" + n], 1)
        if n in HALF:
            SY.dma_start(out[:, col:col + 256], buf[:, col:col + 256]).then_inc(S.st, 16)
            stored += 16
        SY.wait_ge(S["f" + n], 1)
        a = col + (256 if n in HALF else 0)
        SY.dma_start(out[:, a:col + 512], buf[:, a:col + 512]).then_inc(S.st, 16)
        stored += 16
    SY.wait_ge(S.st, stored)
